import numpy as np
import ml_dtypes


def mxq(x, axis, fmt="e4m3"):
    dtype, down = {"e4m3": (ml_dtypes.float8_e4m3fn, 7), "e5m2": (ml_dtypes.float8_e5m2, 14)}[fmt]
    v = np.moveaxis(np.asarray(x, np.float32).astype(ml_dtypes.bfloat16).astype(np.float64), axis, -1)
    blocks = v.reshape(v.shape[:-1] + (-1, 32))
    amax = np.abs(blocks).max(-1, keepdims=True)
    byte = np.maximum(np.where(amax > 0, np.frexp(amax)[1] - 1 + 127, 0) - down, 1)
    scale = np.exp2(byte - 127.0)
    codes = (blocks / scale).astype(np.float32).astype(dtype).astype(np.float64)
    return np.moveaxis((codes * scale).reshape(v.shape), -1, axis)


WIDE = False


def mx_kscale(k):
    if not WIDE:
        return np.ones(k)
    levels = np.array([10, -10, 5, -5, 0])
    if k % 512:
        return np.exp2(np.random.permutation(np.resize(levels, k // 32))).repeat(32)
    a = np.empty((k // 512, 16))
    for p in range(k // 512):
        a[p, :8] = np.random.permutation(np.resize(levels, 8))
        for g in range(8):
            far = levels[np.abs(levels - a[p, g]) >= 10]
            a[p, g + 8] = far[np.random.randint(len(far))]
    return np.exp2(a.ravel()).repeat(32)


BF16 = ml_dtypes.bfloat16


def bf(x):
    return np.asarray(x, np.float32).astype(BF16)


def f64(x):
    return np.asarray(x).astype(np.float64)


E2M1 = np.array([0.0, 0.5, 1.0, 1.5, 2.0, 3.0, 4.0, 6.0, -0.0, -0.5, -1.0, -1.5, -2.0, -3.0, -4.0, -6.0])


def pack_weight(w, fmt):
    k, n = w.shape
    w = f64(bf(w)).reshape(k // 32, 32, n)
    amax = np.abs(w).max(1)
    if fmt == "e4m3":
        byte = np.frexp(amax)[1] - 1 + 127 - 7
    else:
        mant, ex = np.frexp(amax / 6.0)
        byte = np.where(mant > 0.5, ex, ex - 1) + 127
    byte = np.clip(np.where(amax > 0, byte, 1), 1, 254)
    scaled = (w * np.exp2(127.0 - byte)[:, None, :]).reshape(k, n).astype(np.float32)
    by_word = np.ascontiguousarray(scaled.reshape(k // 512, 128, 4, n).transpose(0, 1, 3, 2))
    if fmt == "e4m3":
        words = by_word.astype(ml_dtypes.float8_e4m3fn).view(np.uint8)
    else:
        c = by_word.astype(ml_dtypes.float4_e2m1fn).view(np.uint8) & 0xF
        words = c[..., 0::2] | (c[..., 1::2] << 4)
    return np.ascontiguousarray(words), np.ascontiguousarray(byte.astype(np.uint8).reshape(k // 512, 16, n))


def unpack_weight(words, scales, fmt):
    g, p, n, _ = words.shape
    if fmt == "e4m3":
        vals = np.ascontiguousarray(words).view(ml_dtypes.float8_e4m3fn).astype(np.float64)
    else:
        nib = np.empty((g, p, n, 4), np.uint8)
        nib[..., 0::2] = words & 0xF
        nib[..., 1::2] = words >> 4
        vals = E2M1[nib]
    vals = vals * np.repeat(np.exp2(scales.astype(np.float64) - 127.0), 8, axis=1)[..., None]
    return vals.transpose(0, 1, 3, 2).reshape(g * 512, n)
def pack4(w):
    words, scales = pack_weight(w, "e2m1")
    return words.reshape(words.shape[0], 128, -1), scales


def unpack4(words, scales):
    return unpack_weight(words.reshape(words.shape[0], 128, -1, 2), scales, "e2m1")


def planes(Y):
    n, m = Y.shape
    b = f64(bf(Y)).reshape(n // 32, 32, m)
    amax = np.abs(b).max(1)
    byte = np.clip(np.where(amax > 0, np.frexp(amax)[1] - 1 + 127 - 7, 1), 1, 254)
    codes = (b * np.exp2(127.0 - byte)[:, None, :]).reshape(n, m).astype(np.float32).astype(ml_dtypes.float8_e4m3fn).view(np.uint8)
    words = codes.reshape(n // 512, 128, 4, m).transpose(0, 1, 3, 2)
    return np.ascontiguousarray(words), np.ascontiguousarray(byte.astype(np.uint8).reshape(n // 512, 16, m))


R, C, B = 1536, 1024, 1024


def setup_inputs():
    s1, s2, t = mx_kscale(B), mx_kscale(B), mx_kscale(B)
    A21 = np.random.randn(R, B) * s1[None, :]
    V = np.random.randn(B, B) * B ** -0.75 / s1[:, None]
    W = np.random.randn(B, B) * B ** -0.75 * s2[None, :]
    A12 = np.random.randn(B, C) / s2[:, None]
    dv = np.exp(0.3 * np.random.randn(B)) * t
    dw = np.exp(0.3 * np.random.randn(B)) / t
    A22 = np.random.randn(R, C)
    row_scale = np.exp(0.8 * np.random.randn(R))
    V_words, V_scales = pack4(V)
    A12_words, A12_scales = pack_weight(A12, "e4m3")
    return {"A21": bf(A21), "V_words": V_words, "V_scales": V_scales, "W": bf(W),
            "A12_words": A12_words, "A12_scales": A12_scales, "dv": bf(dv), "dw": bf(dw),
            "A22": bf(A22), "row_scale": bf(row_scale)}

def reference(A21, V_words, V_scales, W, A12_words, A12_scales, dv, dw, A22, row_scale):
    V = unpack4(V_words, V_scales)
    A12 = unpack_weight(A12_words, A12_scales, "e4m3")
    L = (mxq(f64(A21), 1, "e4m3") @ V) * f64(dv)[None, :]
    U = (mxq(f64(W), 1, "e4m3") @ A12) * f64(dw)[:, None]
    y = (f64(A22) - (mxq(L, 1, "e4m3") @ mxq(U, 0, "e4m3"))) * f64(row_scale)[:, None]
    words, scales = planes(y)
    return y, words, scales

from contextlib import ExitStack

import concourse.mybir as mybir
from concourse.masks import make_identity

R, C, B = 1536, 1024, 1024
FLOPS = 2 * R * B * B + 2 * B * B * C + 2 * R * B * C

F32 = mybir.dt.float32
BF16 = mybir.dt.bfloat16
I32 = mybir.dt.int32
U32 = mybir.dt.uint32
U8 = mybir.dt.uint8
FP8X4 = mybir.dt.float8_e4m3fn_x4
FP4X4 = mybir.dt.float4_e2m1fn_x4
COPY = mybir.ActivationFunctionType.Copy
MULT = mybir.AluOpType.mult
ADD = mybir.AluOpType.add

P = 128
SLOTS = 4
GROUP = P * SLOTS
RUN = 8
BANKS = 8
ALIGN = 256
ROW_GROUPS = R // GROUP
RS_ROW = 32
RAW_BUFS = 4
WOVEN_BUFS = 4
PANEL_BUFS = 3
LO, HI, BOTH = (0, GROUP), (GROUP, 2 * GROUP), (0, 2 * GROUP)
ALL = range(SLOTS)


def tile_schur_complement_update_k4_kernel(
    tc, A21, V_words, V_scales, W, A12_words, A12_scales, dv, dw, A22, row_scale, out_0, out_1, out_2
):
    nc = tc.nc
    with ExitStack() as ctx:
        keep = ctx.enter_context(tc.tile_pool(name="keep", bufs=1))
        work = ctx.enter_context(tc.tile_pool(name="work", bufs=1))
        psum = ctx.enter_context(tc.psum_pool(name="psum", bufs=1))
        ctx.enter_context(tc.manual_schedule())

        ident = keep.tile([P, P], F32)
        scales_in = keep.tile([P, 2, 2, B], U8, align_bytes=ALIGN)
        factor_rows = keep.tile([P, GROUP], F32)
        factor_raw = keep.tile([RS_ROW + ROW_GROUPS, GROUP], BF16)
        factors = keep.tile([P, SLOTS, RS_ROW + 4], F32)
        neg_rs = keep.tile([P, SLOTS, 4], F32)
        a12_codes = keep.tile([P, 2, C], U32, align_bytes=ALIGN)
        v_raw = keep.tile([P, 2, B // 2], I32)
        v_codes = keep.tile([P, SLOTS, 2, 2, 2 * P], U8, align_bytes=ALIGN)
        v_scales = keep.tile([P, SLOTS, 2, 2, P], U8, align_bytes=ALIGN)
        w_codes = keep.tile([P, 2, 2 * GROUP], U32, align_bytes=ALIGN)
        w_scales = keep.tile([P, 2, 2 * GROUP], U8, align_bytes=ALIGN)
        a21_codes = keep.tile([P, ROW_GROUPS, 2 * GROUP], U32, align_bytes=ALIGN)
        a21_scales = keep.tile([P, ROW_GROUPS, 2 * GROUP], U8, align_bytes=ALIGN)
        l_codes = keep.tile([P, ROW_GROUPS, 2 * GROUP], U32, align_bytes=ALIGN)
        l_scales = keep.tile([P, ROW_GROUPS, 2 * GROUP], U8, align_bytes=ALIGN)
        u_codes = keep.tile([P, 2, 2 * GROUP], U32, align_bytes=ALIGN)
        u_scales = keep.tile([P, 2, 2 * GROUP], U8, align_bytes=ALIGN)
        y_all = keep.tile([P, ROW_GROUPS, SLOTS, C], F32)
        y_codes = keep.tile([P, ROW_GROUPS, C], U32, align_bytes=ALIGN)
        y_scales = keep.tile([P, ROW_GROUPS, C], U8, align_bytes=ALIGN)
        table_probe = keep.tile([P, 8], F32)
        ones = keep.tile([P, GROUP], BF16, align_bytes=ALIGN)
        ones_codes = keep.tile([P, P], U32, align_bytes=ALIGN)
        ones_scales = keep.tile([P, P], U8, align_bytes=ALIGN)

        quantised = {
            "W": (w_codes, w_scales),
            "A21": (a21_codes, a21_scales),
            "L": (l_codes, l_scales),
            "U": (u_codes, u_scales),
            "Y": (y_codes, y_scales),
        }
        raw, woven, panels, banks_used = {}, {}, {}, []

        def new_bank():
            banks_used.append(len(banks_used) % BANKS)
            return psum.tile([P, GROUP], F32, name="bank%d" % banks_used[-1])

        def group(g):
            return slice(GROUP * g, GROUP * (g + 1))

        def woven_tile(name, n):
            if (name, n) not in woven:
                woven[name, n] = work.tile(
                    [P, 2 * GROUP * SLOTS], BF16, name="woven", bufs=WOVEN_BUFS, align_bytes=ALIGN
                )
            return woven[name, n]

        def copy_on(engine, out, in_):
            if engine == "S":
                nc.scalar.copy(out=out, in_=in_)
            else:
                nc.vector.tensor_copy(out=out, in_=in_)

        def scale_on(engine, out, in_, factor):
            if engine == "S":
                nc.scalar.activation(out=out, in_=in_, func=COPY, scale=factor)
            else:
                nc.vector.tensor_scalar(out=out, in0=in_, scalar1=factor, scalar2=None, op0=MULT)


        def load_w(G, slots):
            if ("W", G) not in raw:
                raw["W", G] = work.tile([P, SLOTS, B], BF16, name="raw", bufs=RAW_BUFS)
            rows = W[group(G), :].rearrange("(b t i) k -> t b i k", t=SLOTS, i=RUN)
            for t in slots:
                nc.sync.dma_start(out=raw["W", G][:, t, :], in_=rows[t])

        def load_rows(name, src, r):
            raw[name, r] = work.tile([P, SLOTS, B], BF16, name="raw", bufs=RAW_BUFS)
            nc.sync.dma_start(out=raw[name, r][:], in_=src[group(r), :].rearrange("(p t) k -> p t k", t=SLOTS))

        def load_a12(c):
            src = A12_words.rearrange("g p n t -> p g (n t)")[:, :, SLOTS * GROUP * c : SLOTS * GROUP * (c + 1)]
            nc.sync.dma_start(out=a12_codes[:, :, group(c)].bitcast(I32), in_=src.bitcast(I32))

        def load_scales(which, src):
            for q in range(4):
                nc.sync.dma_start(
                    out=scales_in[32 * q : 32 * q + 4, which, :, :].bitcast(I32),
                    in_=src[:, 4 * q : 4 * q + 4, :].rearrange("g x n -> x g n").bitcast(I32),
                )

        def load_factors():
            for first, vector in ((0, dv), (2, dw), (RS_ROW, row_scale)):
                rows = vector.rearrange("(g n) -> g n", n=GROUP)
                nc.scalar.dma_start(out=factor_raw[first : first + rows.shape[0], :], in_=rows)


        def order_factors():
            nc.vector.tensor_copy(
                out=factor_rows[0:4, :].rearrange("g (t b i) -> g t b i", t=SLOTS, i=RUN),
                in_=factor_raw[0:4, :].rearrange("g (b t i) -> g t b i", t=SLOTS, i=RUN),
            )
            rs_rows = slice(RS_ROW, RS_ROW + ROW_GROUPS)
            nc.vector.tensor_copy(
                out=factor_rows[rs_rows, :].rearrange("g (t p) -> g t p", t=SLOTS),
                in_=factor_raw[rs_rows, :].rearrange("g (p t) -> g t p", t=SLOTS),
            )

        def turn_factors():
            bank = new_bank()
            for t in ALL:
                nc.tensor.transpose(bank[:, P * t : P * (t + 1)], factor_rows[:, P * t : P * (t + 1)], ident[:])
            turned = bank[:].rearrange("p (t x) -> p t x", t=SLOTS)
            nc.scalar.copy(out=factors[:], in_=turned[:, :, 0 : RS_ROW + 4])
            nc.scalar.activation(out=neg_rs[:], in_=turned[:, :, RS_ROW : RS_ROW + 4], func=COPY, scale=-1.0)

        def order_v():
            nc.vector.tensor_copy(
                out=v_codes[:].rearrange("p t g h n -> p t (g h n)").bitcast(I32).rearrange("p t (b w) -> p t b w", w=4),
                in_=v_raw[:].rearrange("p g (b t w) -> p t (g b) w", t=SLOTS, w=4),
            )
            nc.vector.tensor_copy(
                out=v_scales[:].rearrange("p t g h n -> p t (g h n)").bitcast(I32).rearrange("p t (b w) -> p t b w", w=2),
                in_=scales_in[:, 1, :, :].bitcast(I32).rearrange("p g (b t w) -> p t (g b) w", t=SLOTS, w=2),
            )

        def warm_up(passes):
            bank = new_bank()
            for n in range(passes):
                nc.tensor.matmul_mx(
                    out=bank[:, P * (n % 4) : P * (n % 4 + 1)],
                    lhsT=ones_codes[:].bitcast(FP8X4),
                    lhsT_scale=ones_scales[:],
                    rhs=ones_codes[:].bitcast(FP8X4),
                    rhs_scale=ones_scales[:],
                    start=True,
                    stop=True,
                )


        def turn(bank, quarter, rows, g, u):
            pairs = rows.bitcast(F32)
            nc.tensor.transpose(
                bank[:, P * quarter : P * (quarter + 1)], pairs[:, 2 * P * g + u : 2 * P * (g + 1) : 2], ident[:]
            )

        def turn_w(G, t, engine):
            bank = new_bank()
            for g in range(2):
                for u in range(2):
                    turn(bank, 2 * g + u, raw["W", G][:, t, :], g, u)
            dst = woven_tile("W", G)[:, 2 * GROUP * t : 2 * GROUP * (t + 1)].bitcast(F32)
            copy_on(
                engine,
                dst.rearrange("p (g m u) -> p g m u", g=2, u=2),
                bank[:].rearrange("p (g u m) -> p g m u", g=2, u=2),
            )

        def turn_a21(r, g, engines):
            for h, engine in enumerate(engines):
                bank = new_bank()
                for u in range(2):
                    for s in range(2):
                        turn(bank, 2 * u + s, raw["A21", r][:, 2 * h + s, :], g, u)
                first = 2 * GROUP * (2 * g + h)
                dst = woven_tile("A21", r)[:, first : first + 2 * GROUP].bitcast(F32)
                copy_on(engine, dst.rearrange("p (m u) -> p m u", u=2), bank[:].rearrange("p (u m) -> p m u", u=2))

        def quantise(name, n, columns):
            codes, scales = quantised[name]
            lo, hi = columns
            nc.vector.quantize_mx(
                out=codes[:, n, lo:hi].bitcast(FP8X4),
                scales=scales[:, n, lo:hi],
                in_=woven[name, n][:, SLOTS * lo : SLOTS * hi],
            )

        def quantise_w(G, first, last):
            quantise("W", G, (2 * P * first, 2 * P * (last + 1)))


        def two_passes(operands):
            bank = new_bank()
            for n, (lhs, lhs_scale, rhs, rhs_scale) in enumerate(operands):
                nc.tensor.matmul_mx(
                    out=bank[:], lhsT=lhs, lhsT_scale=lhs_scale, rhs=rhs, rhs_scale=rhs_scale, start=n == 0, stop=n == 1
                )
            return bank

        def panel_out(name, n, G, t, bank, factor, engine):
            if (name, n) not in panels:
                panels[name, n] = work.tile([P, SLOTS, 2 * GROUP], BF16, name="panel", bufs=PANEL_BUFS)
            scale_on(engine, panels[name, n][:, t, group(G)], bank[:], factors[:, t, factor : factor + 1])

        def u_banks(c, G, slots, engine="S"):
            for t in slots:
                cols = [slice(P * (2 * t + g), P * (2 * t + g + 1)) for g in range(2)]
                bank = two_passes(
                    [
                        (
                            w_codes[:, G, cols[g]].bitcast(FP8X4),
                            w_scales[:, G, cols[g]],
                            a12_codes[:, g, group(c)].bitcast(FP8X4),
                            scales_in[:, 0, g, group(c)],
                        )
                        for g in range(2)
                    ]
                )
                panel_out("U", c, G, t, bank, 2 + G, engine)

        def l_banks(r, G, slots, engine="S"):
            for t in slots:
                bank = two_passes(
                    [
                        (
                            v_codes[:, t, g, G, :].bitcast(FP4X4),
                            v_scales[:, t, g, G, :],
                            a21_codes[:, r, group(g)].bitcast(FP8X4),
                            a21_scales[:, r, group(g)],
                        )
                        for g in range(2)
                    ]
                )
                panel_out("L", r, G, t, bank, G, engine)

        def scale_a22(r, slots, engine="V"):
            for t in slots:
                scale_on(engine, y_all[:, r, t, :], raw["A22", r][:, t, :], factors[:, t, RS_ROW + r : RS_ROW + r + 1])

        def y_banks(r, c, slots, slots_a_store=2):
            rows = out_0[group(r), group(c)].rearrange("(p t) m -> p t m", t=SLOTS)
            for t in slots:
                cols = [slice(GROUP * G + P * t, GROUP * G + P * (t + 1)) for G in range(2)]
                bank = two_passes(
                    [
                        (
                            l_codes[:, r, cols[G]].bitcast(FP8X4),
                            l_scales[:, r, cols[G]],
                            u_codes[:, c, group(G)].bitcast(FP8X4),
                            u_scales[:, c, group(G)],
                        )
                        for G in range(2)
                    ]
                )
                y = y_all[:, r, t, group(c)]
                nc.vector.scalar_tensor_tensor(
                    out=y, in0=bank[:], scalar=neg_rs[:, t, r : r + 1], in1=y, op0=MULT, op1=ADD
                )
                if (t + 1) % slots_a_store == 0:
                    done = slice(t + 1 - slots_a_store, t + 1)
                    nc.sync.dma_start(out=rows[:, done, :], in_=y_all[:, r, done, group(c)])

        def interleave(name, n, columns, engine="V"):
            src = y_all[:, n, :, :] if name == "Y" else panels[name, n][:]
            lo, hi = columns
            copy_on(
                engine,
                woven_tile(name, n)[:, SLOTS * lo : SLOTS * hi].rearrange("p (m i t) -> p m t i", i=4, t=SLOTS),
                src[:, :, lo:hi].rearrange("p t (m i) -> p m t i", i=4),
            )

        def quantise_y(r, columns):
            quantise("Y", r, columns)
            lo, hi = columns
            nc.sync.dma_start(
                out=out_1[r].rearrange("p m t -> p (m t)")[:, SLOTS * lo : SLOTS * hi].bitcast(I32),
                in_=y_codes[:, r, lo:hi].bitcast(I32),
            )

        def store_y_scales(lo, hi):
            for q in range(4):
                nc.sync.dma_start(
                    out=out_2[lo:hi, 4 * q : 4 * q + 4, :].rearrange("g x n -> x g n").bitcast(I32),
                    in_=y_scales[32 * q : 32 * q + 4, lo:hi, :].bitcast(I32),
                )

        make_identity(nc, ident[:])
        nc.gpsimd.memset(factor_rows[:], 0.0)
        nc.vector.memset(ones[:], 1.0)
        nc.vector.memset(table_probe[:], 0.0)
        nc.vector.quantize_mx(out=ones_codes[:].bitcast(FP8X4), scales=ones_scales[:], in_=ones[:])
        nc.vector.memset(scales_in[:].rearrange("p a g n -> p (a g n)").bitcast(I32), 0)

        load_factors()
        load_w(0, ALL)
        load_a12(0)
        nc.scalar.activation(out=table_probe[:, 4:5], in_=table_probe[:, 0:1], func=COPY)
        load_scales(0, A12_scales)
        load_w(1, (0, 1))
        load_rows("A22", A22, 0)
        load_w(1, (2, 3))
        load_rows("A21", A21, 0)
        nc.sync.dma_start(out=v_raw[:], in_=V_words.rearrange("g p n -> p g n").bitcast(I32))
        load_scales(1, V_scales)
        load_rows("A21", A21, 1)
        load_rows("A22", A22, 1)
        load_a12(1)
        load_rows("A21", A21, 2)
        load_rows("A22", A22, 2)


        warm_up(8)
        order_factors()
        turn_w(0, 0, "V")
        turn_w(0, 1, "V")
        turn_factors()
        quantise_w(0, 0, 0)
        quantise_w(0, 1, 1)
        turn_w(0, 2, "S")
        turn_w(0, 3, "S")
        quantise_w(0, 2, 2)
        quantise_w(0, 3, 3)
        warm_up(4)
        u_banks(0, 0, (0, 1))
        for t in ALL:
            turn_w(1, t, "S")
        scale_a22(0, (0, 1))
        quantise_w(1, 0, 1)
        scale_a22(0, (2,))
        quantise_w(1, 2, 3)
        scale_a22(0, (3,))
        u_banks(0, 0, (2, 3))
        u_banks(0, 1, (0,))
        interleave("U", 0, LO)
        turn_a21(0, 1, "SS")
        turn_a21(0, 0, "VS")
        order_v()
        quantise("A21", 0, BOTH)
        u_banks(0, 1, (1, 2, 3))
        interleave("U", 0, HI)

        turn_a21(1, 0, "SS")
        turn_a21(1, 1, "SS")
        scale_a22(1, (0, 1))
        quantise("U", 0, BOTH)
        scale_a22(1, (2,))
        l_banks(0, 1, ALL)
        l_banks(0, 0, (0,), "V")
        quantise("A21", 1, BOTH)
        scale_a22(1, (3,))
        l_banks(0, 0, (1, 2, 3))
        interleave("L", 0, BOTH)
        u_banks(1, 0, ALL)
        u_banks(1, 1, (0,))
        u_banks(1, 1, (1,), "V")
        quantise("L", 0, BOTH)
        u_banks(1, 1, (2, 3))
        interleave("U", 1, BOTH)

        l_banks(1, 1, ALL)
        interleave("L", 1, HI, "S")
        y_banks(0, 0, (0,))
        quantise("U", 1, BOTH)
        y_banks(0, 0, (1, 2, 3))
        quantise("L", 1, HI)
        interleave("Y", 0, LO)
        turn_a21(2, 0, "SS")
        turn_a21(2, 1, "SS")
        quantise("A21", 2, BOTH)
        l_banks(1, 0, ALL)
        interleave("L", 1, (GROUP // 2, GROUP), "S")
        y_banks(0, 1, ALL)
        interleave("L", 1, (0, GROUP // 2))
        interleave("Y", 0, HI)
        quantise("L", 1, LO)
        quantise_y(0, BOTH)

        l_banks(2, 1, ALL)
        interleave("L", 2, HI)
        l_banks(2, 0, ALL)
        interleave("L", 2, LO, "S")
        scale_a22(2, ALL, "S")
        y_banks(1, 0, ALL)
        quantise("L", 2, BOTH)
        y_banks(1, 1, ALL)
        interleave("Y", 1, LO, "S")
        interleave("Y", 1, HI, "S")
        y_banks(2, 0, ALL, slots_a_store=1)
        y_banks(2, 1, ALL, slots_a_store=1)

        quarter = C // 4
        quantise_y(1, LO)
        interleave("Y", 2, (0, quarter), "S")
        interleave("Y", 2, (quarter, 2 * quarter))
        quantise_y(1, HI)
        store_y_scales(0, 2)
        interleave("Y", 2, (2 * quarter, 3 * quarter), "S")
        quantise_y(2, LO)
        interleave("Y", 2, (3 * quarter, C))
        quantise_y(2, HI)
        store_y_scales(2, 3)
